import numpy as np
import ml_dtypes


def mxq(x, axis, fmt="e4m3"):
    dtype, down = {"e4m3": (ml_dtypes.float8_e4m3fn, 7), "e5m2": (ml_dtypes.float8_e5m2, 14)}[fmt]
    v = np.moveaxis(np.asarray(x, np.float32).astype(ml_dtypes.bfloat16).astype(np.float64), axis, -1)
    blocks = v.reshape(v.shape[:-1] + (-1, 32))
    amax = np.abs(blocks).max(-1, keepdims=True)
    byte = np.maximum(np.where(amax > 0, np.frexp(amax)[1] - 1 + 127, 0) - down, 1)
    scale = np.exp2(byte - 127.0)
    codes = (blocks / scale).astype(np.float32).astype(dtype).astype(np.float64)
    return np.moveaxis((codes * scale).reshape(v.shape), -1, axis)


WIDE = False


def mx_kscale(k):
    if not WIDE:
        return np.ones(k)
    levels = np.array([10, -10, 5, -5, 0])
    if k % 512:
        return np.exp2(np.random.permutation(np.resize(levels, k // 32))).repeat(32)
    a = np.empty((k // 512, 16))
    for p in range(k // 512):
        a[p, :8] = np.random.permutation(np.resize(levels, 8))
        for g in range(8):
            far = levels[np.abs(levels - a[p, g]) >= 10]
            a[p, g + 8] = far[np.random.randint(len(far))]
    return np.exp2(a.ravel()).repeat(32)


def f64(x):
    return np.asarray(x).astype(np.float64)


def striped(idx):
    return np.tile(idx.reshape(-1, 16).T, (8, 1)).astype(np.uint16)


def unstriped(offs):
    return offs[:16].T.reshape(-1).astype(np.int64)


E2M1 = np.array([0.0, 0.5, 1.0, 1.5, 2.0, 3.0, 4.0, 6.0, -0.0, -0.5, -1.0, -1.5, -2.0, -3.0, -4.0, -6.0])


def pack_weight(w, fmt):
    k, n = w.shape
    w = f64(np.asarray(w, np.float32).astype(ml_dtypes.bfloat16)).reshape(k // 32, 32, n)
    amax = np.abs(w).max(1)
    if fmt == "e4m3":
        byte = np.frexp(amax)[1] - 1 + 127 - 7
    else:
        mant, ex = np.frexp(amax / 6.0)
        byte = np.where(mant > 0.5, ex, ex - 1) + 127
    byte = np.clip(np.where(amax > 0, byte, 1), 1, 254)
    scaled = (w * np.exp2(127.0 - byte)[:, None, :]).reshape(k, n).astype(np.float32)
    by_word = np.ascontiguousarray(scaled.reshape(k // 512, 128, 4, n).transpose(0, 1, 3, 2))
    if fmt == "e4m3":
        words = by_word.astype(ml_dtypes.float8_e4m3fn).view(np.uint8)
    else:
        c = by_word.astype(ml_dtypes.float4_e2m1fn).view(np.uint8) & 0xF
        words = (c[..., 0::2] | (c[..., 1::2] << 4)).reshape(k // 512, 128, 2 * n)
    return np.ascontiguousarray(words), np.ascontiguousarray(byte.astype(np.uint8).reshape(k // 512, 16, n))


def unpack_weight(words, scales, fmt):
    g, _, n = scales.shape
    words = np.ascontiguousarray(words).reshape(g, 128, n, -1)
    if fmt == "e4m3":
        vals = words.view(ml_dtypes.float8_e4m3fn).astype(np.float64)
    else:
        nib = np.empty((g, 128, n, 4), np.uint8)
        nib[..., 0::2] = words & 0xF
        nib[..., 1::2] = words >> 4
        vals = E2M1[nib]
    vals = vals * np.repeat(np.exp2(scales.astype(np.float64) - 127.0), 8, axis=1)[..., None]
    return vals.transpose(0, 1, 3, 2).reshape(g * 512, n)


def gelu(v):
    return 0.5 * v * (1.0 + np.tanh(np.sqrt(2.0 / np.pi) * (v + 0.044715 * v**3)))


K, T, S, P, H = 512, 4096, 1024, 512, 1024


def setup_inputs():
    n = np.random.standard_normal
    s = mx_kscale(K)[:, None]
    u = mx_kscale(H)[:, None]
    tab_words, tab_scales = pack_weight(n((K, T)) * s, "e4m3")
    wa_words, wa_scales = pack_weight(n((K, H)) / np.sqrt(K) / s, "e2m1")
    return {
        "tab_words": tab_words, "tab_scales": tab_scales,
        "offs": striped(np.random.permutation(T)[:S]),
        "pos1": striped(np.random.permutation(S)[:P]),
        "wa_words": wa_words, "wa_scales": wa_scales,
        "wb": (n((K, H)) / np.sqrt(K) / s).astype(np.float32),
        "anilox": (0.8 * n((H, S))).astype(np.float32),
        "gain": (np.exp(0.3 * n(H)) * u[:, 0]).astype(np.float32),
        "wc": (3.0 * n((H, H)) / np.sqrt(H) / u).astype(np.float32),
        "meas": (0.5 * n((H, P))).astype(np.float32),
        "skip": (np.exp(0.3 * n(H)) / u[:, 0]).astype(np.float32),
        "wgo": np.exp(0.3 * n((128, P))).astype(np.float32),
    }


def reference(tab_words, tab_scales, offs, pos1, wa_words, wa_scales, wb,
              anilox, gain, wc, meas, skip, wgo):
    v = unpack_weight(tab_words, tab_scales, "e4m3")[:, unstriped(offs)]
    wa = unpack_weight(wa_words, wa_scales, "e2m1")
    a = wa.T @ v
    b = mxq(f64(wb), 0, "e4m3").T @ v
    h = f64(gain)[:, None] * np.tanh(a * b + f64(anilox))
    x = mxq(h[:, unstriped(pos1)], 0, "e4m3")
    d = mxq(f64(wc), 0, "e4m3").T @ x
    y = 1.0 / (1.0 + np.exp(-d)) + f64(meas)
    out = f64(skip)[:, None] * h
    out[:, unstriped(pos1)] = np.tile(f64(wgo), (H // 128, 1)) * y
    return out

from contextlib import ExitStack

import concourse.mybir as mybir

K, T, S, M, H = 512, 4096, 1024, 512, 1024
FLOPS = 2 * K * H * S * 2 + 2 * H * H * M

F32 = mybir.dt.float32
BF16 = mybir.dt.bfloat16
I32 = mybir.dt.int32
U32 = mybir.dt.uint32
U16 = mybir.dt.uint16
U8 = mybir.dt.uint8
FP8X4 = mybir.dt.float8_e4m3fn_x4
FP4X4 = mybir.dt.float4_e2m1fn_x4
ACT = mybir.ActivationFunctionType
ALU = mybir.AluOpType

P = 128
PACK = 4
PASS = P * PACK
BANK = 512
HALF = M // 2


def tile_list_dot_gain_features_kernel(
    tc, tab_words, tab_scales, offs, pos1, wa_words, wa_scales, wb, anilox, gain, wc, meas, skip, wgo, out
):
    nc = tc.nc
    halves = H // PASS
    row_tiles = [(b, t) for b in range(halves) for t in range(PACK)]
    n = len(row_tiles)

    def rows(dram, b, t):
        return dram[b * PASS : (b + 1) * PASS, :].rearrange("(p t) j -> p t j", t=PACK)[:, t, :]

    with ExitStack() as ctx:
        keep = ctx.enter_context(tc.tile_pool(name="keep", bufs=1))
        ring = ctx.enter_context(tc.tile_pool(name="ring", bufs=3))
        psum = ctx.enter_context(tc.psum_pool(name="psum", bufs=3))

        idx = keep.tile([P, S // 16], U16, name="idx")
        p1 = keep.tile([P, M // 16], U16, name="p1")
        tabw = keep.tile([P, T], U32, name="tabw", align_bytes=64)
        tabs = keep.tile([P, T], U8, name="tabs", align_bytes=64)
        waw_raw = keep.tile([P, 2 * H], U8, name="waw_raw", align_bytes=64)
        was_raw = keep.tile([P, H], U8, name="was_raw", align_bytes=64)
        waw = keep.tile([P, 2 * H], U8, name="waw", align_bytes=64)
        was = keep.tile([P, H], U8, name="was", align_bytes=64)
        gain_t = keep.tile([P, halves, PACK], F32, name="gain_t")
        skip_t = keep.tile([P, halves, PACK], F32, name="skip_t")
        gs = keep.tile([P, halves, PACK], F32, name="gs")
        wgo_t = keep.tile([P, PACK, M], F32, name="wgo_t")

        nc.vector.memset(was_raw[:].bitcast(I32), 0)
        nc.vector.memset(tabs[:].bitcast(I32), 0)

        def load_weight(w, g, b, parts=1):
            raw = []
            width = PASS // parts
            for part in range(parts):
                piece = ring.tile([P, PACK, width], F32, name="raw", bufs=5)
                c0 = b * PASS + part * width
                src = w[g * PASS : (g + 1) * PASS, c0 : c0 + width]
                nc.sync.dma_start(piece[:], src.rearrange("(p j) c -> p j c", j=PACK))
                raw.append(piece)
            return raw

        def load_anilox(i):
            an = keep.tile([P, S], F32, name="an%d" % i)
            nc.sync.dma_start(an[:], rows(anilox, *row_tiles[i]))
            return an

        def on_scalar(dst, src):
            nc.scalar.copy(dst, src)

        def on_vector(dst, src):
            nc.vector.tensor_copy(dst, src)

        def on_gpsimd(dst, src):
            nc.gpsimd.tensor_scalar(dst, src, 1.0, 0.0, ALU.mult, ALU.add)

        def round_weight(raw, cast, rounded=None):
            if rounded is None:
                rounded = ring.tile([P, PASS * PACK], BF16, name="rounded", align_bytes=64, bufs=2)
            dst = rounded[:].rearrange("p (t m j) -> p m j t", t=PACK, j=PACK)
            step = P // 2
            for m0 in range(0, P, step):
                piece = raw[m0 * len(raw) // P]
                first = m0 % (P // len(raw))
                src = piece[:].rearrange("p j (m t) -> p m j t", t=PACK)
                cast(dst[:, m0 : m0 + step], src[:, first : first + step])
            return rounded

        def quantise(rounded, width, name):
            codes = keep.tile([P, width], U32, name=name + "_codes", align_bytes=64)
            scales = keep.tile([P, width], U8, name=name + "_scales", align_bytes=64)
            nc.vector.quantize_mx(out=codes[:].bitcast(FP8X4), scales=scales[:], in_=rounded)
            return codes, scales

        nc.sync.dma_start(idx[:], offs)
        nc.sync.dma_start(tabw[:].bitcast(I32), tab_words[0].rearrange("p n t -> p (n t)").bitcast(I32))
        nc.scalar.dma_start(waw_raw[:].bitcast(I32), wa_words[0].bitcast(I32))
        for q in range(4):
            nc.scalar.dma_start(
                was_raw[32 * q : 32 * q + 4, :].bitcast(I32), wa_scales[0, 4 * q : 4 * q + 4, :].bitcast(I32)
            )
        for q in range(4):
            nc.sync.dma_start(
                tabs[32 * q : 32 * q + 4, :].bitcast(I32), tab_scales[0, 4 * q : 4 * q + 4, :].bitcast(I32)
            )
        wb_raw = {0: load_weight(wb, 0, 0, parts=2)}
        an = {0: load_anilox(0)}
        wb_raw[1] = load_weight(wb, 0, 1)
        nc.sync.dma_start(p1[:], pos1)
        nc.sync.dma_start(gain_t[:], gain.rearrange("(b p t) -> p b t", p=P, t=PACK))
        nc.sync.dma_start(skip_t[:], skip.rearrange("(b p t) -> p b t", p=P, t=PACK))
        an[1] = load_anilox(1)
        an[2] = load_anilox(2)
        an[3] = load_anilox(3)
        wc_raw = {(0, 0): load_weight(wc, 0, 0)}
        an[4] = load_anilox(4)
        an[5] = load_anilox(5)
        wc_raw[1, 0] = load_weight(wc, 1, 0)
        an[6] = load_anilox(6)
        an[7] = load_anilox(7)
        for q in (0, 2, 1, 3):
            nc.sync.dma_start(wgo_t[32 * q : 32 * q + 32], wgo.rearrange("(p t) m -> p t m", t=PACK))
        meas_t = {}
        for b in range(halves):
            meas_t[b] = keep.tile([P, PACK, M], F32, name="meas%d" % b)
        nc.sync.dma_start(meas_t[0][:], meas[0:PASS, :].rearrange("(p t) m -> p t m", t=PACK))
        wc_raw[0, 1] = load_weight(wc, 0, 1)
        wc_raw[1, 1] = load_weight(wc, 1, 1)
        nc.sync.dma_start(meas_t[1][:], meas[PASS : 2 * PASS, :].rearrange("(p t) m -> p t m", t=PACK))

        nc.vector.tensor_copy(
            waw[:].rearrange("p (b t m e) -> p b t m e", b=halves, t=PACK, e=2),
            waw_raw[:].rearrange("p (b m t e) -> p b t m e", b=halves, t=PACK, e=2),
        )
        nc.vector.tensor_copy(
            was[:].rearrange("p (b t m) -> p b t m", b=halves, t=PACK),
            was_raw[:].rearrange("p (b m t) -> p b t m", b=halves, t=PACK),
        )

        v_words, v_scales = [], []
        for u in range(S // BANK):
            cols = idx[:, u * (BANK // 16) : (u + 1) * (BANK // 16)]
            vw = keep.tile([P, BANK], U32, name="vw%d" % u, align_bytes=64)
            vs = keep.tile([P, BANK], U8, name="vs%d" % u, align_bytes=64)
            nc.vector.tensor_copy(vw[:], tabw[:].indirect(cols))
            nc.vector.tensor_copy(vs[:], tabs[:].indirect(cols))
            v_words.append(vw)
            v_scales.append(vs)

        wb_q = {0: quantise(round_weight(wb_raw[0], on_scalar)[:], PASS, "wb0")}
        nc.vector.tensor_tensor(gs[:], gain_t[:], skip_t[:], ALU.mult)

        tanh_t, picked, x_q, wc_q, woven = {}, {}, {}, {}, {}

        def first_stage(i):
            b, t = row_tiles[i]
            codes, scales = wb_q[b]
            prod = ring.tile([P, S], F32, name="prod", bufs=2)
            for u in range(S // BANK):
                pa = psum.tile([P, BANK], F32, name="pa")
                pb = psum.tile([P, BANK], F32, name="pb")
                nc.tensor.matmul_mx(
                    out=pa[:],
                    lhsT=waw[:, 2 * P * i : 2 * P * (i + 1)].bitcast(FP4X4),
                    lhsT_scale=was[:, P * i : P * (i + 1)],
                    rhs=v_words[u][:].bitcast(FP8X4),
                    rhs_scale=v_scales[u][:],
                    start=True,
                    stop=True,
                )
                nc.tensor.matmul_mx(
                    out=pb[:],
                    lhsT=codes[:, P * t : P * (t + 1)].bitcast(FP8X4),
                    lhsT_scale=scales[:, P * t : P * (t + 1)],
                    rhs=v_words[u][:].bitcast(FP8X4),
                    rhs_scale=v_scales[u][:],
                    start=True,
                    stop=True,
                )
                a_sb = ring.tile([P, BANK], F32, name="a_sb")
                nc.scalar.copy(a_sb[:], pa[:])
                nc.vector.tensor_tensor(prod[:, u * BANK : (u + 1) * BANK], pb[:], a_sb[:], ALU.mult)
            return prod

        def shift_and_tanh(i, prod):
            z = an[i]
            tanh_t[i] = keep.tile([P, S], F32, name="tanh%d" % i)
            for c0 in range(0, S, 1024):
                cols = slice(c0, c0 + 1024)
                nc.vector.tensor_tensor(z[:, cols], prod[:, cols], z[:, cols], ALU.add)
                nc.scalar.activation(tanh_t[i][:, cols], z[:, cols], ACT.Tanh)

        def pick(i, c0, c1):
            b, t = row_tiles[i]
            if b not in picked:
                picked[b] = keep.tile([P, PACK, M], BF16, name="picked%d" % b)
            g = ring.tile([P, c1 - c0], F32, name="g")
            nc.vector.tensor_copy(g[:], tanh_t[i][:].indirect(p1[:, c0 // 16 : c1 // 16]))
            nc.scalar.activation(picked[b][:, t, c0:c1], g[:], ACT.Copy, scale=gain_t[:, b, t : t + 1])

        def weave(b, c0, c1):
            if b not in woven:
                woven[b] = keep.tile([P, M * PACK], BF16, name="woven%d" % b, align_bytes=64)
            part = woven[b][:, c0 * PACK : c1 * PACK]
            nc.vector.tensor_copy(
                part.rearrange("p (c i t) -> p c t i", i=4, t=PACK),
                picked[b][:, :, c0:c1].rearrange("p t (c i) -> p c t i", i=4),
            )
            return part

        prods = {}
        for step in range(n + 1):
            if step < n:
                prods[step] = first_stage(step)
            if step >= 1:
                shift_and_tanh(step - 1, prods[step - 1])
            if step >= 2:
                pick(step - 2, 0, M)
            if step == 2:
                wb_q[1] = quantise(round_weight(wb_raw[1], on_scalar)[:], PASS, "wb1")
            if step == 4:
                wc_q[0, 0] = quantise(round_weight(wc_raw[0, 0], on_scalar)[:], PASS, "wc00")
            if step == 6:
                wc_q[1, 0] = quantise(round_weight(wc_raw[1, 0], on_scalar)[:], PASS, "wc10")
                x_q[0] = quantise(weave(0, 0, M), M, "x0")
        pick(n - 1, 0, HALF)
        pick(n - 1, HALF, M)
        x1 = [quantise(weave(1, c0, c0 + HALF), HALF, "x1_%d" % c0) for c0 in (0, HALF)]

        pages = {}

        def fill_page(i):
            b, t = row_tiles[i]
            pages[i] = keep.tile([P, S], F32, name="page%d" % i, tag="an%d" % (n - 3 + i % 3))
            nc.scalar.activation(pages[i][:], tanh_t[i][:], ACT.Copy, scale=gs[:, b, t : t + 1])

        def second_stage(i, c0, c1):
            b, t = row_tiles[i]
            pd = psum.tile([P, c1 - c0], F32, name="pd", bufs=2)
            passes = [(0, 0, c1 - c0, x_q[0][0][:, c0:c1], x_q[0][1][:, c0:c1])]
            for h0 in range(c0, c1, HALF):
                passes.append((1, h0 - c0, h0 - c0 + HALF, x1[h0 // HALF][0][:], x1[h0 // HALF][1][:]))
            for k, (g, d0, d1, x_codes, x_scales) in enumerate(passes):
                codes, scales = wc_q[g, b]
                nc.tensor.matmul_mx(
                    out=pd[:, d0:d1],
                    lhsT=codes[:, P * t : P * (t + 1)].bitcast(FP8X4),
                    lhsT_scale=scales[:, P * t : P * (t + 1)],
                    rhs=x_codes.bitcast(FP8X4),
                    rhs_scale=x_scales,
                    start=(k == 0),
                    stop=(k == len(passes) - 1),
                )
            sig = ring.tile([P, c1 - c0], F32, name="sig")
            nc.scalar.activation(sig[:], pd[:], ACT.Sigmoid)
            y = ring.tile([P, c1 - c0], F32, name="y")
            nc.vector.tensor_tensor(y[:], sig[:], meas_t[b][:, t, c0:c1], ALU.add)
            return y

        def put(i, c0, c1, y):
            b, t = row_tiles[i]
            window = pages[i][:].indirect(p1[:, c0 // 16 : c1 // 16])
            nc.vector.tensor_tensor(window, y[:], wgo_t[:, t, c0:c1], ALU.mult)
            if c1 == M:
                nc.sync.dma_start(rows(out, b, t), pages[i][:])

        units = [(0, 0, HALF), (0, HALF, M)] + [(i, 0, M) for i in range(1, n)]
        fill_page(0)
        staged = second_stage(*units[0])
        for k, unit in enumerate(units):
            ready = staged
            if k + 1 < len(units):
                staged = second_stage(*units[k + 1])
                if units[k + 1][1] == 0:
                    fill_page(units[k + 1][0])
            put(*unit, ready)
            if k in (1, 2):
                g = k - 1
                wc_q[g, 1] = quantise(round_weight(wc_raw[g, 1], on_scalar, woven[1])[:], PASS, "wc%d1" % g)
